import numpy as np
import ml_dtypes


def mxq(x, axis, fmt="e4m3"):
    dtype, down = {"e4m3": (ml_dtypes.float8_e4m3fn, 7), "e5m2": (ml_dtypes.float8_e5m2, 14)}[fmt]
    v = np.moveaxis(np.asarray(x, np.float32).astype(ml_dtypes.bfloat16).astype(np.float64), axis, -1)
    blocks = v.reshape(v.shape[:-1] + (-1, 32))
    amax = np.abs(blocks).max(-1, keepdims=True)
    byte = np.maximum(np.where(amax > 0, np.frexp(amax)[1] - 1 + 127, 0) - down, 1)
    scale = np.exp2(byte - 127.0)
    codes = (blocks / scale).astype(np.float32).astype(dtype).astype(np.float64)
    return np.moveaxis((codes * scale).reshape(v.shape), -1, axis)


WIDE = False


def mx_kscale(k):
    if not WIDE:
        return np.ones(k)
    levels = np.array([10, -10, 5, -5, 0])
    if k % 512:
        return np.exp2(np.random.permutation(np.resize(levels, k // 32))).repeat(32)
    a = np.empty((k // 512, 16))
    for p in range(k // 512):
        a[p, :8] = np.random.permutation(np.resize(levels, 8))
        for g in range(8):
            far = levels[np.abs(levels - a[p, g]) >= 10]
            a[p, g + 8] = far[np.random.randint(len(far))]
    return np.exp2(a.ravel()).repeat(32)


def f64(x):
    return np.asarray(x).astype(np.float64)


def striped(idx):
    return np.tile(np.asarray(idx).reshape(-1, 16).T, (8, 1)).astype(np.uint16)


def unstriped(offs):
    return offs[:16].T.reshape(-1).astype(np.int64)


E2M1 = np.array([0.0, 0.5, 1.0, 1.5, 2.0, 3.0, 4.0, 6.0, -0.0, -0.5, -1.0, -1.5, -2.0, -3.0, -4.0, -6.0])


def pack_weight(w, fmt):
    k, n = w.shape
    w = f64(np.asarray(w, np.float32).astype(ml_dtypes.bfloat16)).reshape(k // 32, 32, n)
    amax = np.abs(w).max(1)
    if fmt == "e4m3":
        byte = np.frexp(amax)[1] - 1 + 127 - 7
    else:
        mant, ex = np.frexp(amax / 6.0)
        byte = np.where(mant > 0.5, ex, ex - 1) + 127
    byte = np.clip(np.where(amax > 0, byte, 1), 1, 254)
    scaled = (w * np.exp2(127.0 - byte)[:, None, :]).reshape(k, n).astype(np.float32)
    by_word = np.ascontiguousarray(scaled.reshape(k // 512, 128, 4, n).transpose(0, 1, 3, 2))
    if fmt == "e4m3":
        words = by_word.astype(ml_dtypes.float8_e4m3fn).view(np.uint8)
    else:
        c = by_word.astype(ml_dtypes.float4_e2m1fn).view(np.uint8) & 0xF
        words = (c[..., 0::2] | (c[..., 1::2] << 4)).reshape(k // 512, 128, 2 * n)
    return np.ascontiguousarray(words), np.ascontiguousarray(byte.astype(np.uint8).reshape(k // 512, 16, n))


def unpack_weight(words, scales, fmt):
    g, _, n = scales.shape
    words = np.ascontiguousarray(words).reshape(g, 128, n, -1)
    if fmt == "e4m3":
        vals = words.view(ml_dtypes.float8_e4m3fn).astype(np.float64)
    else:
        nib = np.empty((g, 128, n, 4), np.uint8)
        nib[..., 0::2] = words & 0xF
        nib[..., 1::2] = words >> 4
        vals = E2M1[nib]
    vals = vals * np.repeat(np.exp2(scales.astype(np.float64) - 127.0), 8, axis=1)[..., None]
    return vals.transpose(0, 1, 3, 2).reshape(g * 512, n)


D, T, U, I, J, G = 512, 1024, 1024, 256, 512, 64


def setup_inputs():
    n = np.random.standard_normal
    idx = np.random.permutation(T)[:I]
    idx2 = np.random.permutation(U)[:J]
    fd = mx_kscale(D)
    tabbp = pack_weight(n((D, U)) / fd[:, None], "e4m3")
    return {
        "taba": (n((D, T)) * 1 / np.sqrt(D) * fd[:, None]).astype(np.float32),
        "tabb_words": tabbp[0],
        "tabb_scales": tabbp[1],
        "gw": (np.random.uniform(0.5, 2.0, (I, G))).astype(np.float32),
        "old": (0.3 * n((I, J))).astype(np.float32),
        "offs": striped(idx),
        "offs2": striped(idx2),
    }


def reference(taba, tabb_words, tabb_scales, gw, old, offs, offs2):
    idx = unstriped(offs)
    idx2 = unstriped(offs2)
    tabbu = unpack_weight(tabb_words, tabb_scales, "e4m3")
    tabaidxq = mxq(f64(taba)[:, idx], 0, "e4m3")
    tabbidx2g = tabbu[:, idx2]
    s = tabaidxq.T @ tabbidx2g
    b = s - np.max(s, axis=1, keepdims=True)
    p = np.exp(b)
    z = np.sum(p, axis=1, keepdims=True)
    s1g = p.reshape(I, G, J // G).sum(axis=2)
    ds1g = f64(gw) / (s1g / z + 0.002) / z
    r1 = np.repeat(ds1g, J // G, axis=1)
    dz = np.sum(f64(gw) / (s1g / z + 0.002) * s1g / np.square(z) * (-1.0), axis=1, keepdims=True)
    dp = r1 + dz
    db = dp * p
    y = db * 4.0 + f64(old)
    return y

@@ -1,0 +1,129 @@
+from contextlib import ExitStack
+
+import concourse.mybir as mybir
+
+F32 = mybir.dt.float32
+BF16 = mybir.dt.bfloat16
+I32 = mybir.dt.int32
+U32 = mybir.dt.uint32
+U16 = mybir.dt.uint16
+U8 = mybir.dt.uint8
+FP8X4 = mybir.dt.float8_e4m3fn_x4
+ALU = mybir.AluOpType
+ACT = mybir.ActivationFunctionType
+AX = mybir.AxisListType
+
+P = 128
+D, T, U, I, J, G = 512, 1024, 1024, 256, 512, 64
+PACK = 4
+R = J // G
+H = I // P
+FLOPS = 2 * D * I * J
+
+
+def tile_attend_bgrouplogshare_kernel(tc, taba, tabb_words, tabb_scales, gw, old, offs, offs2, out):
+    nc = tc.nc
+    with ExitStack() as ctx:
+        keep = ctx.enter_context(tc.tile_pool(name="keep", bufs=1))
+        psum = ctx.enter_context(tc.psum_pool(name="psum", bufs=1))
+
+        list_a = keep.tile([P, I // 16], U16, name="list_a")
+        list_b = keep.tile([P, J // 16], U16, name="list_b")
+        scale_win = keep.tile([P, U], U8, name="scale_win", tag="scales_then_gw", align_bytes=64)
+        word_win = keep.tile([P, U], I32, name="word_win", tag="words_then_old", align_bytes=64)
+        a_win = [keep.tile([P, T], F32, name=f"a_win{t}", align_bytes=64) for t in range(PACK)]
+
+        nc.gpsimd.memset(scale_win[:].bitcast(I32), 0)
+        nc.sync.dma_start(list_b[:], offs2)
+        nc.sync.dma_start(word_win[:], tabb_words[0].rearrange("p n t -> p (n t)").bitcast(I32))
+        nc.sync.dma_start(list_a[:], offs)
+        scale_rows = tabb_scales[0].bitcast(I32)
+        for q, queue in enumerate((nc.sync, nc.sync, nc.sync, nc.sync)):
+            queue.dma_start(scale_win[32 * q : 32 * q + 4, :].bitcast(I32), scale_rows[4 * q : 4 * q + 4, :])
+        planes = taba.rearrange("(p t) n -> p t n", t=PACK)
+        for t in range(PACK):
+            nc.sync.dma_start(a_win[t][:], planes[:, t, :])
+
+        sums = [keep.tile([P, G + 1], F32, name=f"sums{h}") for h in range(H)]
+        for h in range(H):
+            nc.vector.memset(sums[h][:, G : G + 1], 0.0)
+
+        b_codes = keep.tile([P, J], U32, name="b_codes", align_bytes=64)
+        nc.vector.tensor_copy(b_codes[:], word_win[:].bitcast(U32).indirect(list_b[:]))
+        early = keep.tile([P, 2, I], F32, name="early", align_bytes=64)
+        nc.vector.tensor_copy(early[:, 0, :], a_win[0][:].indirect(list_a[:]))
+        b_scales = keep.tile([P, J], U8, name="b_scales", align_bytes=64)
+        nc.vector.tensor_copy(b_scales[:], scale_win[:].indirect(list_b[:]))
+        nc.vector.tensor_copy(early[:, 1, :], a_win[1][:].indirect(list_a[:]))
+
+        gw_sb = keep.tile([P, H, G], F32, name="gw_sb", tag="scales_then_gw", align_bytes=64)
+        old_sb = keep.tile([P, H, J], F32, name="old_sb", tag="words_then_old", align_bytes=64)
+        nc.sync.dma_start(old_sb[:], old.rearrange("(h p) j -> p h j", p=P))
+        nc.sync.dma_start(gw_sb[:], gw.rearrange("(h p) g -> p h g", p=P))
+
+        grouped = [keep.tile([P, P, PACK], BF16, name=f"grouped{h}", align_bytes=64) for h in range(H)]
+        for h in range(H):
+            nc.scalar.activation(
+                grouped[h][:, :, 0:2], early[:, :, h * P : (h + 1) * P].rearrange("p t i -> p i t"), ACT.Copy
+            )
+        for t in (2, 3):
+            for h in range(H):
+                nc.vector.tensor_copy(grouped[h][:, :, t], a_win[t][:].indirect(list_a[:, 8 * h : 8 * h + 8]))
+
+        gw_scaled = keep.tile([P, H, G], F32, name="gw_scaled")
+        nc.scalar.activation(gw_scaled[:], gw_sb[:], ACT.Copy, scale=2000.0)
+
+        s = []
+        for h in range(H):
+            a_codes = keep.tile([P, P], U32, name=f"a_codes{h}", align_bytes=64)
+            a_scales = keep.tile([P, P], U8, name=f"a_scales{h}", align_bytes=64)
+            nc.vector.quantize_mx(
+                out=a_codes[:].bitcast(FP8X4), scales=a_scales[:], in_=grouped[h][:].rearrange("p i t -> p (i t)")
+            )
+            s.append(psum.tile([P, J], F32, name=f"s{h}"))
+            nc.tensor.matmul_mx(
+                out=s[h][:],
+                lhsT=a_codes[:].bitcast(FP8X4),
+                lhsT_scale=a_scales[:],
+                rhs=b_codes[:].bitcast(FP8X4),
+                rhs_scale=b_scales[:],
+                start=True,
+                stop=True,
+            )
+
+        def per_tile(name, width):
+            return [keep.tile([P, width], F32, name=f"{name}{h}") for h in range(H)]
+
+        neg_max, z, dz = per_tile("neg_max", 1), per_tile("z", 1), per_tile("dz", 1)
+        p, db, y = per_tile("p", J), per_tile("db", J), per_tile("y", J)
+        denom, inv = per_tile("denom", G + 1), per_tile("inv", G + 1)
+        a, terms, gw_sums = per_tile("a", G), per_tile("terms", G), per_tile("gw_sums", G)
+        p_g = [p[h][:].rearrange("p (g r) -> p g r", r=R) for h in range(H)]
+        for h in range(H):
+            nc.vector.tensor_reduce(neg_max[h][:], s[h][:], AX.X, ALU.max, negate=True)
+            nc.scalar.activation(p[h][:], s[h][:], ACT.Exp, bias=neg_max[h][:], accum_out=z[h][:])
+        for h in range(H):
+            nc.vector.tensor_reduce(sums[h][:, 0:G], p_g[h], AX.X, ALU.add)
+            nc.vector.tensor_scalar(denom[h][:], sums[h][:], 500.0, z[h][:], ALU.mult, ALU.add)
+            nc.vector.tensor_tensor(gw_sums[h][:], sums[h][:, 0:G], gw_scaled[:, h, :], ALU.mult)
+        for h in range(H):
+            nc.vector.reciprocal(inv[h][:], denom[h][:])
+            nc.vector.tensor_tensor(a[h][:], inv[h][:, 0:G], gw_scaled[:, h, :], ALU.mult)
+            nc.vector.scalar_tensor_tensor(
+                terms[h][:], inv[h][:, 0:G], inv[h][:, G : G + 1], gw_sums[h][:], ALU.mult, ALU.mult, accum_out=dz[h][:]
+            )
+        for h in range(H):
+            nc.vector.scalar_tensor_tensor(
+                db[h][:].rearrange("p (g r) -> p g r", r=R),
+                a[h][:].unsqueeze(2).to_broadcast([P, G, R]),
+                dz[h][:],
+                p_g[h],
+                ALU.subtract,
+                ALU.mult,
+            )
+            pieces = 2 if h == H - 1 else 1
+            width = J // pieces
+            for c in range(pieces):
+                cols = slice(c * width, (c + 1) * width)
+                nc.vector.tensor_tensor(y[h][:, cols], db[h][:, cols], old_sb[:, h, cols], ALU.add)
+                nc.sync.dma_start(out[h * P : (h + 1) * P, cols], y[h][:, cols])

@@ -31,18 +31,20 @@ def tile_attend_bgrouplogshare_kernel(tc, taba, tabb_words, tabb_scales, gw, old
         list_b = keep.tile([P, J // 16], U16, name="list_b")
         scale_win = keep.tile([P, U], U8, name="scale_win", tag="scales_then_gw", align_bytes=64)
         word_win = keep.tile([P, U], I32, name="word_win", tag="words_then_old", align_bytes=64)
-        a_win = [keep.tile([P, T], F32, name=f"a_win{t}", align_bytes=64) for t in range(PACK)]
+        first_win = keep.tile([P, 2, T], F32, name="first_win", align_bytes=64)
+        late_win = [keep.tile([P, T], F32, name=f"late_win{t}", align_bytes=64) for t in range(2)]
 
         nc.gpsimd.memset(scale_win[:].bitcast(I32), 0)
-        nc.sync.dma_start(list_b[:], offs2)
         nc.sync.dma_start(word_win[:], tabb_words[0].rearrange("p n t -> p (n t)").bitcast(I32))
+        nc.sync.dma_start(list_b[:], offs2)
         nc.sync.dma_start(list_a[:], offs)
         scale_rows = tabb_scales[0].bitcast(I32)
         for q, queue in enumerate((nc.sync, nc.sync, nc.sync, nc.sync)):
             queue.dma_start(scale_win[32 * q : 32 * q + 4, :].bitcast(I32), scale_rows[4 * q : 4 * q + 4, :])
         planes = taba.rearrange("(p t) n -> p t n", t=PACK)
-        for t in range(PACK):
-            nc.sync.dma_start(a_win[t][:], planes[:, t, :])
+        nc.sync.dma_start(first_win[:], planes[:, 0:2, :])
+        for t in range(2):
+            nc.sync.dma_start(late_win[t][:], planes[:, 2 + t, :])
 
         sums = [keep.tile([P, G + 1], F32, name=f"sums{h}") for h in range(H)]
         for h in range(H):
@@ -51,10 +53,10 @@ def tile_attend_bgrouplogshare_kernel(tc, taba, tabb_words, tabb_scales, gw, old
         b_codes = keep.tile([P, J], U32, name="b_codes", align_bytes=64)
         nc.vector.tensor_copy(b_codes[:], word_win[:].bitcast(U32).indirect(list_b[:]))
         early = keep.tile([P, 2, I], F32, name="early", align_bytes=64)
-        nc.vector.tensor_copy(early[:, 0, :], a_win[0][:].indirect(list_a[:]))
         b_scales = keep.tile([P, J], U8, name="b_scales", align_bytes=64)
         nc.vector.tensor_copy(b_scales[:], scale_win[:].indirect(list_b[:]))
-        nc.vector.tensor_copy(early[:, 1, :], a_win[1][:].indirect(list_a[:]))
+        for t in range(2):
+            nc.vector.tensor_copy(early[:, t, :], first_win[:, t, :].indirect(list_a[:]))
 
         gw_sb = keep.tile([P, H, G], F32, name="gw_sb", tag="scales_then_gw", align_bytes=64)
         old_sb = keep.tile([P, H, J], F32, name="old_sb", tag="words_then_old", align_bytes=64)
@@ -68,7 +70,7 @@ def tile_attend_bgrouplogshare_kernel(tc, taba, tabb_words, tabb_scales, gw, old
             )
         for t in (2, 3):
             for h in range(H):
-                nc.vector.tensor_copy(grouped[h][:, :, t], a_win[t][:].indirect(list_a[:, 8 * h : 8 * h + 8]))
+                nc.vector.tensor_copy(grouped[h][:, :, t], late_win[t - 2][:].indirect(list_a[:, 8 * h : 8 * h + 8]))
 
         gw_scaled = keep.tile([P, H, G], F32, name="gw_scaled")
         nc.scalar.activation(gw_scaled[:], gw_sb[:], ACT.Copy, scale=2000.0)
@@ -106,24 +108,24 @@ def tile_attend_bgrouplogshare_kernel(tc, taba, tabb_words, tabb_scales, gw, old
             nc.vector.tensor_reduce(sums[h][:, 0:G], p_g[h], AX.X, ALU.add)
             nc.vector.tensor_scalar(denom[h][:], sums[h][:], 500.0, z[h][:], ALU.mult, ALU.add)
             nc.vector.tensor_tensor(gw_sums[h][:], sums[h][:, 0:G], gw_scaled[:, h, :], ALU.mult)
-        for h in range(H):
             nc.vector.reciprocal(inv[h][:], denom[h][:])
-            nc.vector.tensor_tensor(a[h][:], inv[h][:, 0:G], gw_scaled[:, h, :], ALU.mult)
             nc.vector.scalar_tensor_tensor(
                 terms[h][:], inv[h][:, 0:G], inv[h][:, G : G + 1], gw_sums[h][:], ALU.mult, ALU.mult, accum_out=dz[h][:]
             )
-        for h in range(H):
-            nc.vector.scalar_tensor_tensor(
-                db[h][:].rearrange("p (g r) -> p g r", r=R),
-                a[h][:].unsqueeze(2).to_broadcast([P, G, R]),
-                dz[h][:],
-                p_g[h],
-                ALU.subtract,
-                ALU.mult,
-            )
-            pieces = 2 if h == H - 1 else 1
-            width = J // pieces
+            nc.vector.tensor_tensor(a[h][:], inv[h][:, 0:G], gw_scaled[:, h, :], ALU.mult)
+            pieces = 2
+            groups = G // pieces
             for c in range(pieces):
-                cols = slice(c * width, (c + 1) * width)
+                gs = slice(c * groups, (c + 1) * groups)
+                nc.vector.scalar_tensor_tensor(
+                    db[h][:].rearrange("p (g r) -> p g r", r=R)[:, gs, :],
+                    a[h][:, gs].unsqueeze(2).to_broadcast([P, groups, R]),
+                    dz[h][:],
+                    p_g[h][:, gs, :],
+                    ALU.subtract,
+                    ALU.mult,
+                )
+            for c in range(pieces):
+                cols = slice(c * groups * R, (c + 1) * groups * R)
                 nc.vector.tensor_tensor(y[h][:, cols], db[h][:, cols], old_sb[:, h, cols], ALU.add)
                 nc.sync.dma_start(out[h * P : (h + 1) * P, cols], y[h][:, cols])

@@ -31,32 +31,34 @@ def tile_attend_bgrouplogshare_kernel(tc, taba, tabb_words, tabb_scales, gw, old
         list_b = keep.tile([P, J // 16], U16, name="list_b")
         scale_win = keep.tile([P, U], U8, name="scale_win", tag="scales_then_gw", align_bytes=64)
         word_win = keep.tile([P, U], I32, name="word_win", tag="words_then_old", align_bytes=64)
-        first_win = keep.tile([P, 2, T], F32, name="first_win", align_bytes=64)
-        late_win = [keep.tile([P, T], F32, name=f"late_win{t}", align_bytes=64) for t in range(2)]
+        a_win = [keep.tile([P, T], F32, name=f"a_win{t}", align_bytes=64) for t in range(PACK)]
 
         nc.gpsimd.memset(scale_win[:].bitcast(I32), 0)
-        nc.sync.dma_start(word_win[:], tabb_words[0].rearrange("p n t -> p (n t)").bitcast(I32))
+        planes = taba.rearrange("(p t) n -> p t n", t=PACK)
         nc.sync.dma_start(list_b[:], offs2)
+        nc.sync.dma_start(a_win[0][:], planes[:, 0, :])
         nc.sync.dma_start(list_a[:], offs)
         scale_rows = tabb_scales[0].bitcast(I32)
-        for q, queue in enumerate((nc.sync, nc.sync, nc.sync, nc.sync)):
-            queue.dma_start(scale_win[32 * q : 32 * q + 4, :].bitcast(I32), scale_rows[4 * q : 4 * q + 4, :])
-        planes = taba.rearrange("(p t) n -> p t n", t=PACK)
-        nc.sync.dma_start(first_win[:], planes[:, 0:2, :])
-        for t in range(2):
-            nc.sync.dma_start(late_win[t][:], planes[:, 2 + t, :])
+        for q in range(4):
+            nc.sync.dma_start(scale_win[32 * q : 32 * q + 4, :].bitcast(I32), scale_rows[4 * q : 4 * q + 4, :])
+        nc.sync.dma_start(word_win[:], tabb_words[0].rearrange("p n t -> p (n t)").bitcast(I32))
+        for t in range(1, PACK):
+            nc.sync.dma_start(a_win[t][:], planes[:, t, :])
 
         sums = [keep.tile([P, G + 1], F32, name=f"sums{h}") for h in range(H)]
         for h in range(H):
             nc.vector.memset(sums[h][:, G : G + 1], 0.0)
 
-        b_codes = keep.tile([P, J], U32, name="b_codes", align_bytes=64)
-        nc.vector.tensor_copy(b_codes[:], word_win[:].bitcast(U32).indirect(list_b[:]))
-        early = keep.tile([P, 2, I], F32, name="early", align_bytes=64)
+        early = keep.tile([P, 2, I], BF16, name="early", align_bytes=64)
+        plane0 = keep.tile([P, T], BF16, name="plane0", align_bytes=64)
+        nc.scalar.activation(plane0[:], a_win[0][:], ACT.Copy)
+        nc.scalar.activation(early[:, 0, :], plane0[:].indirect(list_a[:]), ACT.Copy)
+
         b_scales = keep.tile([P, J], U8, name="b_scales", align_bytes=64)
         nc.vector.tensor_copy(b_scales[:], scale_win[:].indirect(list_b[:]))
-        for t in range(2):
-            nc.vector.tensor_copy(early[:, t, :], first_win[:, t, :].indirect(list_a[:]))
+        b_codes = keep.tile([P, J], U32, name="b_codes", align_bytes=64)
+        nc.vector.tensor_copy(b_codes[:], word_win[:].bitcast(U32).indirect(list_b[:]))
+        nc.vector.tensor_copy(early[:, 1, :], a_win[1][:].indirect(list_a[:]))
 
         gw_sb = keep.tile([P, H, G], F32, name="gw_sb", tag="scales_then_gw", align_bytes=64)
         old_sb = keep.tile([P, H, J], F32, name="old_sb", tag="words_then_old", align_bytes=64)
@@ -70,7 +72,7 @@ def tile_attend_bgrouplogshare_kernel(tc, taba, tabb_words, tabb_scales, gw, old
             )
         for t in (2, 3):
             for h in range(H):
-                nc.vector.tensor_copy(grouped[h][:, :, t], late_win[t - 2][:].indirect(list_a[:, 8 * h : 8 * h + 8]))
+                nc.vector.tensor_copy(grouped[h][:, :, t], a_win[t][:].indirect(list_a[:, 8 * h : 8 * h + 8]))
 
         gw_scaled = keep.tile([P, H, G], F32, name="gw_scaled")
         nc.scalar.activation(gw_scaled[:], gw_sb[:], ACT.Copy, scale=2000.0)

@@ -34,30 +34,26 @@ def tile_attend_bgrouplogshare_kernel(tc, taba, tabb_words, tabb_scales, gw, old
         a_win = [keep.tile([P, T], F32, name=f"a_win{t}", align_bytes=64) for t in range(PACK)]
 
         nc.gpsimd.memset(scale_win[:].bitcast(I32), 0)
-        planes = taba.rearrange("(p t) n -> p t n", t=PACK)
         nc.sync.dma_start(list_b[:], offs2)
-        nc.sync.dma_start(a_win[0][:], planes[:, 0, :])
+        nc.sync.dma_start(word_win[:], tabb_words[0].rearrange("p n t -> p (n t)").bitcast(I32))
         nc.sync.dma_start(list_a[:], offs)
         scale_rows = tabb_scales[0].bitcast(I32)
-        for q in range(4):
-            nc.sync.dma_start(scale_win[32 * q : 32 * q + 4, :].bitcast(I32), scale_rows[4 * q : 4 * q + 4, :])
-        nc.sync.dma_start(word_win[:], tabb_words[0].rearrange("p n t -> p (n t)").bitcast(I32))
-        for t in range(1, PACK):
+        for q, queue in enumerate((nc.sync, nc.sync, nc.sync, nc.sync)):
+            queue.dma_start(scale_win[32 * q : 32 * q + 4, :].bitcast(I32), scale_rows[4 * q : 4 * q + 4, :])
+        planes = taba.rearrange("(p t) n -> p t n", t=PACK)
+        for t in range(PACK):
             nc.sync.dma_start(a_win[t][:], planes[:, t, :])
 
         sums = [keep.tile([P, G + 1], F32, name=f"sums{h}") for h in range(H)]
         for h in range(H):
             nc.vector.memset(sums[h][:, G : G + 1], 0.0)
 
-        early = keep.tile([P, 2, I], BF16, name="early", align_bytes=64)
-        plane0 = keep.tile([P, T], BF16, name="plane0", align_bytes=64)
-        nc.scalar.activation(plane0[:], a_win[0][:], ACT.Copy)
-        nc.scalar.activation(early[:, 0, :], plane0[:].indirect(list_a[:]), ACT.Copy)
-
-        b_scales = keep.tile([P, J], U8, name="b_scales", align_bytes=64)
-        nc.vector.tensor_copy(b_scales[:], scale_win[:].indirect(list_b[:]))
         b_codes = keep.tile([P, J], U32, name="b_codes", align_bytes=64)
         nc.vector.tensor_copy(b_codes[:], word_win[:].bitcast(U32).indirect(list_b[:]))
+        early = keep.tile([P, 2, I], F32, name="early", align_bytes=64)
+        nc.vector.tensor_copy(early[:, 0, :], a_win[0][:].indirect(list_a[:]))
+        b_scales = keep.tile([P, J], U8, name="b_scales", align_bytes=64)
+        nc.vector.tensor_copy(b_scales[:], scale_win[:].indirect(list_b[:]))
         nc.vector.tensor_copy(early[:, 1, :], a_win[1][:].indirect(list_a[:]))
 
         gw_sb = keep.tile([P, H, G], F32, name="gw_sb", tag="scales_then_gw", align_bytes=64)
@@ -108,13 +104,15 @@ def tile_attend_bgrouplogshare_kernel(tc, taba, tabb_words, tabb_scales, gw, old
             nc.scalar.activation(p[h][:], s[h][:], ACT.Exp, bias=neg_max[h][:], accum_out=z[h][:])
         for h in range(H):
             nc.vector.tensor_reduce(sums[h][:, 0:G], p_g[h], AX.X, ALU.add)
-            nc.vector.tensor_scalar(denom[h][:], sums[h][:], 500.0, z[h][:], ALU.mult, ALU.add)
+            nc.scalar.activation(denom[h][:], sums[h][:], ACT.Identity, bias=z[h][:], scale=500.0)
             nc.vector.tensor_tensor(gw_sums[h][:], sums[h][:, 0:G], gw_scaled[:, h, :], ALU.mult)
+        for h in range(H):
             nc.vector.reciprocal(inv[h][:], denom[h][:])
             nc.vector.scalar_tensor_tensor(
                 terms[h][:], inv[h][:, 0:G], inv[h][:, G : G + 1], gw_sums[h][:], ALU.mult, ALU.mult, accum_out=dz[h][:]
             )
             nc.vector.tensor_tensor(a[h][:], inv[h][:, 0:G], gw_scaled[:, h, :], ALU.mult)
+        for h in range(H):
             pieces = 2
             groups = G // pieces
             for c in range(pieces):
@@ -130,4 +128,7 @@ def tile_attend_bgrouplogshare_kernel(tc, taba, tabb_words, tabb_scales, gw, old
             for c in range(pieces):
                 cols = slice(c * groups * R, (c + 1) * groups * R)
                 nc.vector.tensor_tensor(y[h][:, cols], db[h][:, cols], old_sb[:, h, cols], ALU.add)
-                nc.sync.dma_start(out[h * P : (h + 1) * P, cols], y[h][:, cols])
+                if h == H - 1:
+                    nc.sync.dma_start(out[h * P : (h + 1) * P, cols], y[h][:, cols])
+            if h < H - 1:
+                nc.sync.dma_start(out[h * P : (h + 1) * P, :], y[h][:])

@@ -50,8 +50,10 @@ def tile_attend_bgrouplogshare_kernel(tc, taba, tabb_words, tabb_scales, gw, old
 
         b_codes = keep.tile([P, J], U32, name="b_codes", align_bytes=64)
         nc.vector.tensor_copy(b_codes[:], word_win[:].bitcast(U32).indirect(list_b[:]))
-        early = keep.tile([P, 2, I], F32, name="early", align_bytes=64)
-        nc.vector.tensor_copy(early[:, 0, :], a_win[0][:].indirect(list_a[:]))
+        early = keep.tile([P, 2, I], BF16, name="early", align_bytes=64)
+        plane0 = keep.tile([P, T], BF16, name="plane0", align_bytes=64)
+        nc.scalar.activation(plane0[:], a_win[0][:], ACT.Copy)
+        nc.scalar.activation(early[:, 0, :], plane0[:].indirect(list_a[:]), ACT.Copy)
         b_scales = keep.tile([P, J], U8, name="b_scales", align_bytes=64)
         nc.vector.tensor_copy(b_scales[:], scale_win[:].indirect(list_b[:]))
         nc.vector.tensor_copy(early[:, 1, :], a_win[1][:].indirect(list_a[:]))

from contextlib import ExitStack

import concourse.mybir as mybir

F32 = mybir.dt.float32
BF16 = mybir.dt.bfloat16
I32 = mybir.dt.int32
U32 = mybir.dt.uint32
U16 = mybir.dt.uint16
U8 = mybir.dt.uint8
FP8X4 = mybir.dt.float8_e4m3fn_x4
ALU = mybir.AluOpType
ACT = mybir.ActivationFunctionType
AX = mybir.AxisListType

P = 128
D, T, U, I, J, G = 512, 1024, 1024, 256, 512, 64
PACK = 4
R = J // G
H = I // P
FLOPS = 2 * D * I * J


def tile_attend_bgrouplogshare_kernel(tc, taba, tabb_words, tabb_scales, gw, old, offs, offs2, out):
    nc = tc.nc
    with ExitStack() as ctx:
        keep = ctx.enter_context(tc.tile_pool(name="keep", bufs=1))
        psum = ctx.enter_context(tc.psum_pool(name="psum", bufs=1))

        list_a = keep.tile([P, I // 16], U16, name="list_a")
        list_b = keep.tile([P, J // 16], U16, name="list_b")
        scale_win = keep.tile([P, U], U8, name="scale_win", tag="scales_then_gw", align_bytes=64)
        word_win = keep.tile([P, U], I32, name="word_win", tag="words_then_old", align_bytes=64)
        a_win = [keep.tile([P, T], F32, name=f"a_win{t}", align_bytes=64) for t in range(PACK)]

        nc.gpsimd.memset(scale_win[:].bitcast(I32), 0)
        nc.sync.dma_start(list_b[:], offs2)
        nc.sync.dma_start(word_win[:], tabb_words[0].rearrange("p n t -> p (n t)").bitcast(I32))
        nc.sync.dma_start(list_a[:], offs)
        scale_rows = tabb_scales[0].bitcast(I32)
        for q, queue in enumerate((nc.sync, nc.sync, nc.sync, nc.sync)):
            queue.dma_start(scale_win[32 * q : 32 * q + 4, :].bitcast(I32), scale_rows[4 * q : 4 * q + 4, :])
        planes = taba.rearrange("(p t) n -> p t n", t=PACK)
        for t in range(PACK):
            nc.sync.dma_start(a_win[t][:], planes[:, t, :])

        sums = [keep.tile([P, G + 1], F32, name=f"sums{h}") for h in range(H)]
        for h in range(H):
            nc.vector.memset(sums[h][:, G : G + 1], 0.0)

        b_codes = keep.tile([P, J], U32, name="b_codes", align_bytes=64)
        nc.vector.tensor_copy(b_codes[:], word_win[:].bitcast(U32).indirect(list_b[:]))
        early = keep.tile([P, 2, I], BF16, name="early", align_bytes=64)
        plane0 = keep.tile([P, T], BF16, name="plane0", align_bytes=64)
        nc.scalar.activation(plane0[:], a_win[0][:], ACT.Copy)
        nc.scalar.activation(early[:, 0, :], plane0[:].indirect(list_a[:]), ACT.Copy)
        b_scales = keep.tile([P, J], U8, name="b_scales", align_bytes=64)
        nc.vector.tensor_copy(b_scales[:], scale_win[:].indirect(list_b[:]))
        nc.vector.tensor_copy(early[:, 1, :], a_win[1][:].indirect(list_a[:]))

        gw_sb = keep.tile([P, H, G], F32, name="gw_sb", tag="scales_then_gw", align_bytes=64)
        old_sb = keep.tile([P, H, J], F32, name="old_sb", tag="words_then_old", align_bytes=64)
        nc.sync.dma_start(old_sb[:], old.rearrange("(h p) j -> p h j", p=P))
        nc.sync.dma_start(gw_sb[:], gw.rearrange("(h p) g -> p h g", p=P))

        grouped = [keep.tile([P, P, PACK], BF16, name=f"grouped{h}", align_bytes=64) for h in range(H)]
        for h in range(H):
            nc.scalar.activation(
                grouped[h][:, :, 0:2], early[:, :, h * P : (h + 1) * P].rearrange("p t i -> p i t"), ACT.Copy
            )
        for t in (2, 3):
            for h in range(H):
                nc.vector.tensor_copy(grouped[h][:, :, t], a_win[t][:].indirect(list_a[:, 8 * h : 8 * h + 8]))

        gw_scaled = keep.tile([P, H, G], F32, name="gw_scaled")
        nc.scalar.activation(gw_scaled[:], gw_sb[:], ACT.Copy, scale=2000.0)

        s = []
        for h in range(H):
            a_codes = keep.tile([P, P], U32, name=f"a_codes{h}", align_bytes=64)
            a_scales = keep.tile([P, P], U8, name=f"a_scales{h}", align_bytes=64)
            nc.vector.quantize_mx(
                out=a_codes[:].bitcast(FP8X4), scales=a_scales[:], in_=grouped[h][:].rearrange("p i t -> p (i t)")
            )
            s.append(psum.tile([P, J], F32, name=f"s{h}"))
            nc.tensor.matmul_mx(
                out=s[h][:],
                lhsT=a_codes[:].bitcast(FP8X4),
                lhsT_scale=a_scales[:],
                rhs=b_codes[:].bitcast(FP8X4),
                rhs_scale=b_scales[:],
                start=True,
                stop=True,
            )

        def per_tile(name, width):
            return [keep.tile([P, width], F32, name=f"{name}{h}") for h in range(H)]

        neg_max, z, dz = per_tile("neg_max", 1), per_tile("z", 1), per_tile("dz", 1)
        p, db, y = per_tile("p", J), per_tile("db", J), per_tile("y", J)
        denom, inv = per_tile("denom", G + 1), per_tile("inv", G + 1)
        a, terms, gw_sums = per_tile("a", G), per_tile("terms", G), per_tile("gw_sums", G)
        p_g = [p[h][:].rearrange("p (g r) -> p g r", r=R) for h in range(H)]
        for h in range(H):
            nc.vector.tensor_reduce(neg_max[h][:], s[h][:], AX.X, ALU.max, negate=True)
            nc.scalar.activation(p[h][:], s[h][:], ACT.Exp, bias=neg_max[h][:], accum_out=z[h][:])
        for h in range(H):
            nc.vector.tensor_reduce(sums[h][:, 0:G], p_g[h], AX.X, ALU.add)
            nc.scalar.activation(denom[h][:], sums[h][:], ACT.Identity, bias=z[h][:], scale=500.0)
            nc.vector.tensor_tensor(gw_sums[h][:], sums[h][:, 0:G], gw_scaled[:, h, :], ALU.mult)
        for h in range(H):
            nc.vector.reciprocal(inv[h][:], denom[h][:])
            nc.vector.scalar_tensor_tensor(
                terms[h][:], inv[h][:, 0:G], inv[h][:, G : G + 1], gw_sums[h][:], ALU.mult, ALU.mult, accum_out=dz[h][:]
            )
            nc.vector.tensor_tensor(a[h][:], inv[h][:, 0:G], gw_scaled[:, h, :], ALU.mult)
        for h in range(H):
            pieces = 2
            groups = G // pieces
            for c in range(pieces):
                gs = slice(c * groups, (c + 1) * groups)
                nc.vector.scalar_tensor_tensor(
                    db[h][:].rearrange("p (g r) -> p g r", r=R)[:, gs, :],
                    a[h][:, gs].unsqueeze(2).to_broadcast([P, groups, R]),
                    dz[h][:],
                    p_g[h][:, gs, :],
                    ALU.subtract,
                    ALU.mult,
                )
            for c in range(pieces):
                cols = slice(c * groups * R, (c + 1) * groups * R)
                nc.vector.tensor_tensor(y[h][:, cols], db[h][:, cols], old_sb[:, h, cols], ALU.add)
                if h == H - 1:
                    nc.sync.dma_start(out[h * P : (h + 1) * P, cols], y[h][:, cols])
            if h < H - 1:
                nc.sync.dma_start(out[h * P : (h + 1) * P, :], y[h][:])
